import numpy as np
import ml_dtypes


def mxq(x, axis, fmt="e4m3"):
    dtype, down = {"e4m3": (ml_dtypes.float8_e4m3fn, 7), "e5m2": (ml_dtypes.float8_e5m2, 14)}[fmt]
    v = np.moveaxis(np.asarray(x, np.float32).astype(ml_dtypes.bfloat16).astype(np.float64), axis, -1)
    blocks = v.reshape(v.shape[:-1] + (-1, 32))
    amax = np.abs(blocks).max(-1, keepdims=True)
    byte = np.maximum(np.where(amax > 0, np.frexp(amax)[1] - 1 + 127, 0) - down, 1)
    scale = np.exp2(byte - 127.0)
    codes = (blocks / scale).astype(np.float32).astype(dtype).astype(np.float64)
    return np.moveaxis((codes * scale).reshape(v.shape), -1, axis)


WIDE = False


def mx_kscale(k):
    if not WIDE:
        return np.ones(k)
    levels = np.array([10, -10, 5, -5, 0])
    if k % 512:
        return np.exp2(np.random.permutation(np.resize(levels, k // 32))).repeat(32)
    a = np.empty((k // 512, 16))
    for p in range(k // 512):
        a[p, :8] = np.random.permutation(np.resize(levels, 8))
        for g in range(8):
            far = levels[np.abs(levels - a[p, g]) >= 10]
            a[p, g + 8] = far[np.random.randint(len(far))]
    return np.exp2(a.ravel()).repeat(32)


def f64(x):
    return np.asarray(x).astype(np.float64)


def striped(idx):
    return np.tile(idx.reshape(-1, 16).T, (8, 1)).astype(np.uint16)


def unstriped(offs):
    return offs[:16].T.reshape(-1).astype(np.int64)


def striped8(idx):
    return np.concatenate([x.reshape(-1, 16).T for x in idx]).astype(np.uint16)


def runs(offs, k):
    lists = np.stack([offs[16 * r : 16 * r + 16].T.reshape(-1) for r in range(8)]).astype(np.int64)
    return lists[np.arange(k) % 512 // 64]


def pack_weight(w):
    k, n = w.shape
    w = f64(np.asarray(w, np.float32).astype(ml_dtypes.bfloat16)).reshape(k // 32, 32, n)
    amax = np.abs(w).max(1)
    byte = np.clip(np.where(amax > 0, np.frexp(amax)[1] - 1 + 127 - 7, 1), 1, 254)
    scaled = (w * np.exp2(127.0 - byte)[:, None, :]).reshape(k, n).astype(np.float32)
    words = np.ascontiguousarray(scaled.reshape(k // 512, 128, 4, n).transpose(0, 1, 3, 2)).astype(ml_dtypes.float8_e4m3fn).view(np.uint8)
    return words, np.ascontiguousarray(byte.astype(np.uint8).reshape(k // 512, 16, n))


def unpack_weight(words, scales):
    g, p, n, _ = words.shape
    vals = np.ascontiguousarray(words).view(ml_dtypes.float8_e4m3fn).astype(np.float64) * np.repeat(np.exp2(scales.astype(np.float64) - 127.0), 8, axis=1)[..., None]
    return vals.transpose(0, 1, 3, 2).reshape(g * 512, n)


K, T, S, N, G, H = 512, 2048, 256, 512, 2048, 512


def setup_inputs():
    n = np.random.standard_normal
    s = mx_kscale(K)[:, None]
    u = mx_kscale(K)
    packed_xT = pack_weight(n((K, T)) * s)
    packed_dT = pack_weight(n((K, G)) / s)
    return {
        "x_words": packed_xT[0],
        "x_scales": packed_xT[1],
        "d_words": packed_dT[0],
        "d_scales": packed_dT[1],
        "gn": (np.random.uniform(0.5, 1.5, (H, 1)) * u[:, None]).astype(np.float32),
        "w1": (n((H, N)) / np.sqrt(2 * H) / u[:, None]).astype(np.float32),
        "w2": (n((K, N)) / np.sqrt(2 * K) / s).astype(np.float32),
        "offs": striped(np.random.permutation(T)[:S]),
        "k1": striped8(np.random.randint(0, G, (8, H))),
        "two": striped(np.random.permutation(T)[:S]),
        "n1": striped(np.random.permutation(S)),
        "n2": striped(np.random.permutation(S)),
    }


def reference(x_words, x_scales, d_words, d_scales, gn, w1, w2, offs, k1, two, n1, n2):
    d_k1 = unpack_weight(d_words, d_scales)[np.arange(K)[:, None], runs(k1, K)]
    xq = unpack_weight(x_words, x_scales)[:, unstriped(offs)]
    s = 0.0625 * (d_k1.T @ xq)
    z = f64(gn) * s
    x_two = unpack_weight(x_words, x_scales)[:, unstriped(two)]
    h = mxq(f64(w1), 0, "e4m3").T @ mxq(z, 0, "e4m3") + mxq(f64(w2), 0, "e4m3").T @ x_two
    ds = np.zeros((N, S))
    ds[:, unstriped(n1)] = h
    return np.maximum(h, ds[:, unstriped(n2)])

@@ -1,0 +1,245 @@
+from contextlib import ExitStack
+
+import concourse.mybir as mybir
+
+K, T, S, N, G, H = 512, 2048, 256, 512, 2048, 512
+FLOPS = 2 * K * H * S + 2 * H * N * S + 2 * K * N * S
+
+F32 = mybir.dt.float32
+BF16 = mybir.dt.bfloat16
+I32 = mybir.dt.int32
+U32 = mybir.dt.uint32
+U16 = mybir.dt.uint16
+U8 = mybir.dt.uint8
+FP8X4 = mybir.dt.float8_e4m3fn_x4
+MULT = mybir.AluOpType.mult
+MAX = mybir.AluOpType.max
+COPY = mybir.ActivationFunctionType.Copy
+
+P = 128
+PACK = 4
+HALF = S // 2
+TILES = N // P
+
+
+def tile_picked_kmixirelay_none_p_kernel(
+    tc, x_words, x_scales, d_words, d_scales, gn, w1, w2, offs, k1, two, n1, n2, out
+):
+    nc = tc.nc
+    with ExitStack() as ctx:
+        lists = ctx.enter_context(tc.tile_pool(name="lists", bufs=1))
+        pool = ctx.enter_context(tc.tile_pool(name="pool", bufs=1))
+        psum = ctx.enter_context(tc.psum_pool(name="psum", bufs=1))
+
+        k1_t = lists.tile([P, H // 16], U16, name="k1_t")
+        offs_t = lists.tile([P, S // 16], U16, name="offs_t")
+        two_t = lists.tile([P, S // 16], U16, name="two_t")
+        n1_t = lists.tile([P, S // 16], U16, name="n1_t")
+        n2_t = lists.tile([P, S // 16], U16, name="n2_t")
+
+        d_bytes = pool.tile([P, G], U8, name="d_bytes", align_bytes=64)
+        x_bytes = pool.tile([P, T], U8, name="x_bytes", align_bytes=64)
+        placed = pool.tile([P, H + 2 * S], U8, name="placed", align_bytes=64)
+        nc.vector.memset(placed[:].bitcast(I32), 0)
+        ds = [pool.tile([P, 2 * S], F32, name=f"ds{u}") for u in range(TILES)]
+        for u in range(TILES):
+            nc.vector.memset(ds[u][:, S:], 0.0)
+
+        d_tab = pool.tile([P, G], I32, name="d_tab", align_bytes=64)
+        x_tab = pool.tile([P, T], I32, name="x_tab", align_bytes=64)
+        gain = pool.tile([P, PACK], F32, name="gain")
+
+        def load_scale_rows(table, scales):
+            rows = scales[0].bitcast(I32)
+            nc.sync.dma_start(table[:].bitcast(I32), rows.unsqueeze(1).to_broadcast([16, 8, rows.shape[1]]))
+
+        nc.sync.dma_start(k1_t[:], k1)
+        load_scale_rows(d_bytes, d_scales)
+        nc.sync.dma_start(offs_t[:], offs)
+        nc.sync.dma_start(two_t[:], two)
+        load_scale_rows(x_bytes, x_scales)
+        nc.sync.dma_start(d_tab[:], d_words[0].rearrange("p n t -> p (n t)").bitcast(I32))
+        nc.sync.dma_start(n1_t[:], n1)
+        nc.sync.dma_start(n2_t[:], n2)
+        nc.sync.dma_start(x_tab[:], x_words[0].rearrange("p n t -> p (n t)").bitcast(I32))
+        nc.gpsimd.dma_start(gain[:], gn.rearrange("(p t) o -> p (t o)", t=PACK))
+
+        raw = {}
+
+        def load_w(u, i):
+            raw[u, i] = pool.tile([P, PACK, P], F32, name=f"raw{u}{i}", tag=f"raw{u}{i}")[:]
+            w = (w2, w1)[i]
+            nc.sync.dma_start(raw[u, i], w[:, u * P : (u + 1) * P].rearrange("(p j) n -> p j n", j=PACK))
+
+        load_w(0, 0)
+
+        picked = pool.tile([P, H + 2 * S], U8, name="picked", align_bytes=64)
+        dealt = pool.tile([P, H + 2 * S], U8, name="dealt", align_bytes=64)
+
+        def gather_keys(table, gathered, target, run):
+            for b in range(2):
+                nc.vector.tensor_copy(
+                    gathered[:, b * H // 2 : (b + 1) * H // 2], table.indirect(k1_t[:, b * H // 32 : (b + 1) * H // 32])
+                )
+            for b in range(2):
+                nc.vector.tensor_copy(
+                    target.rearrange("p (t b c i) -> p b c t i", t=PACK, b=2, i=run)[:, b],
+                    gathered[:, b * H // 2 : (b + 1) * H // 2].rearrange("p (c i t) -> p c t i", t=PACK, i=run),
+                )
+
+        gather_keys(d_bytes[:], picked[:, 0:H], dealt[:, 0:H], 16)
+        nc.vector.tensor_copy(picked[:, H : H + S], x_bytes[:].indirect(offs_t[:]))
+        nc.vector.tensor_copy(picked[:, H + S :], x_bytes[:].indirect(two_t[:]))
+        nc.vector.tensor_copy(dealt[:, H:].bitcast(I32), picked[:, H:].bitcast(I32))
+        for a in range(PACK):
+            queue = nc.sync if a % 2 == 0 else nc.scalar
+            queue.dma_start(placed[a:P:32, :].bitcast(I32), dealt[8 * a : P : 32, :].bitcast(I32))
+
+        load_w(0, 1)
+        for u in range(1, TILES):
+            load_w(u, 0)
+            load_w(u, 1)
+
+        keys = pool.tile([P, H], U32, name="keys", align_bytes=64)
+        key_words = pool.tile([P, H], U32, name="key_words", align_bytes=64)
+        gather_keys(d_tab[:].bitcast(U32), keys[:], key_words[:], 4)
+        xo = pool.tile([P, S], U32, name="xo", align_bytes=64)
+        xt = pool.tile([P, S], U32, name="xt", align_bytes=64)
+        halves = [slice(0, HALF), slice(HALF, S)]
+        cols16 = [slice(0, HALF // 16), slice(HALF // 16, S // 16)]
+        nc.vector.tensor_copy(xo[:, halves[0]], x_tab[:].bitcast(U32).indirect(offs_t[:, cols16[0]]))
+        key_scales = placed[:, 0:H]
+        nc.vector.tensor_copy(xo[:, halves[1]], x_tab[:].bitcast(U32).indirect(offs_t[:, cols16[1]]))
+        nc.vector.tensor_copy(xt[:], x_tab[:].bitcast(U32).indirect(two_t[:]))
+        xo_scales = placed[:, H : H + S]
+        xt_scales = placed[:, H + S :]
+
+        s_banks = [psum.tile([P, PACK, HALF], F32, name=f"s{b}") for b in range(2)]
+        for b in range(2):
+            for t in range(PACK):
+                nc.tensor.matmul_mx(
+                    s_banks[b][:, t, :],
+                    lhsT=key_words[:, t * P : (t + 1) * P].bitcast(FP8X4),
+                    lhsT_scale=key_scales[:, t * P : (t + 1) * P],
+                    rhs=xo[:, halves[b]].bitcast(FP8X4),
+                    rhs_scale=xo_scales[:, halves[b]],
+                    start=True,
+                    stop=True,
+                )
+
+        w_bf = {}
+        z_bf = {}
+
+        def staged(width, name, slot):
+            return pool.tile([P, width], BF16, name=name, tag=f"staged{slot}", align_bytes=64)
+
+        w_q = [pool.tile([P, 2 * P], U32, name=f"w_q{u}", tag=f"w_q{u}", align_bytes=64) for u in range(TILES)]
+        w_s = [pool.tile([P, 2 * P], U8, name=f"w_s{u}", align_bytes=64) for u in range(TILES)]
+
+        def cast(copy, u, i):
+            copy(
+                w_bf[u, i].rearrange("p (c n j) -> p c j n", j=PACK, n=4),
+                raw[u, i].rearrange("p j (c n) -> p c j n", n=4),
+            )
+
+        def quantise_w(u, lo, hi, source):
+            nc.vector.quantize_mx(w_q[u][:, lo * P : hi * P].bitcast(FP8X4), w_s[u][:, lo * P : hi * P], source)
+
+        z_q = pool.tile([P, S], U32, name="z_q", align_bytes=64)
+        z_s = pool.tile([P, S], U8, name="z_s", align_bytes=64)
+
+        def make_z(b):
+            nc.vector.scalar_tensor_tensor(
+                z_bf[b].rearrange("p (n t) -> p n t", t=PACK),
+                s_banks[b][:].rearrange("p t n -> p n t"),
+                0.0625,
+                gain[:].unsqueeze(1).to_broadcast([P, HALF, PACK]),
+                MULT,
+                MULT,
+            )
+
+        def quantise_z(b):
+            nc.vector.quantize_mx(
+                z_q[:, halves[b]].bitcast(FP8X4),
+                z_s[:, halves[b]],
+                z_bf[b],
+            )
+
+        def product(acc, u, cols):
+            nc.tensor.matmul_mx(
+                acc,
+                lhsT=w_q[u][:, 0:P].bitcast(FP8X4),
+                lhsT_scale=w_s[u][:, 0:P],
+                rhs=xt[:, cols].bitcast(FP8X4),
+                rhs_scale=xt_scales[:, cols],
+                start=True,
+                stop=False,
+            )
+            nc.tensor.matmul_mx(
+                acc,
+                lhsT=w_q[u][:, P : 2 * P].bitcast(FP8X4),
+                lhsT_scale=w_s[u][:, P : 2 * P],
+                rhs=z_q[:, cols].bitcast(FP8X4),
+                rhs_scale=z_s[:, cols],
+                start=False,
+                stop=True,
+            )
+
+        h = [pool.tile([P, S], F32, name=f"h{u}") for u in range(TILES)]
+        fetched = {}
+
+        def fetch(u, tag):
+            fetched[u] = pool.tile([P, S], F32, name=f"fetched{u}", tag=tag)
+            nc.scalar.activation(fetched[u][:], ds[u][:].indirect(n2_t[:]), COPY)
+
+        def finish(u):
+            nc.vector.tensor_tensor(res[:, u * S : (u + 1) * S], h[u][:], fetched[u][:], MAX)
+            nc.sync.dma_start(out[u * P : (u + 1) * P, :], res[:, u * S : (u + 1) * S])
+
+        width = P * PACK
+        both = staged(2 * width, "w_bf0", 0)
+        w_bf[0, 0], w_bf[0, 1] = both[:, :width], both[:, width:]
+        z_bf[0] = staged(width, "z_bf0", 1)[:]
+        cast(nc.scalar.copy, 0, 0)
+        cast(nc.scalar.copy, 0, 1)
+        make_z(0)
+        quantise_w(0, 0, 1, w_bf[0, 0])
+        quantise_z(0)
+        quantise_w(0, 1, 2, w_bf[0, 1])
+        first = [psum.tile([P, HALF], F32, name=f"first{b}") for b in range(2)]
+        product(first[0][:], 0, halves[0])
+        nc.scalar.copy(h[0][:, halves[0]], first[0][:])
+        nc.scalar.activation(ds[0][:].indirect(n1_t[:, cols16[0]]), h[0][:, halves[0]], COPY)
+        w_bf[1, 0] = staged(width, "w_bf10", 1)[:]
+        cast(nc.scalar.copy, 1, 0)
+        both = staged(2 * width, "z_bf1_w_bf11", 0)
+        z_bf[1], w_bf[1, 1] = both[:, :width], both[:, width:]
+        make_z(1)
+        cast(nc.vector.tensor_copy, 1, 1)
+        quantise_z(1)
+        product(first[1][:], 0, halves[1])
+        quantise_w(1, 0, 1, w_bf[1, 0])
+        quantise_w(1, 1, 2, w_bf[1, 1])
+        nc.vector.tensor_copy(h[0][:, halves[1]], first[1][:])
+        nc.scalar.activation(ds[0][:].indirect(n1_t[:, cols16[1]]), h[0][:, halves[1]], COPY)
+        for u in range(1, TILES):
+            acc = psum.tile([P, S], F32, name=f"acc{u}")
+            product(acc[:], u, slice(0, S))
+            if u + 1 < TILES:
+                both = staged(2 * width, f"w_bf{u + 1}", 0)
+                w_bf[u + 1, 0], w_bf[u + 1, 1] = both[:, :width], both[:, width:]
+                cast(nc.vector.tensor_copy, u + 1, 0)
+            nc.vector.tensor_copy(h[u][:], acc[:])
+            if u + 1 < TILES:
+                cast(nc.vector.tensor_copy, u + 1, 1)
+                quantise_w(u + 1, 0, 2, both[:])
+            nc.scalar.activation(ds[u][:].indirect(n1_t[:]), h[u][:], COPY)
+            if u + 1 < TILES:
+                fetch(u - 1, f"raw{u + 1}1")
+        res = pool.tile([P, TILES * S], F32, name="res", tag=f"w_q{TILES - 1}", align_bytes=64)
+        finish(0)
+        fetch(2, "raw21")
+        finish(1)
+        fetch(3, "raw31")
+        finish(2)
+        finish(3)

@@ -39,8 +39,10 @@ def tile_picked_kmixirelay_none_p_kernel(
 
         d_bytes = pool.tile([P, G], U8, name="d_bytes", align_bytes=64)
         x_bytes = pool.tile([P, T], U8, name="x_bytes", align_bytes=64)
-        placed = pool.tile([P, H + 2 * S], U8, name="placed", align_bytes=64)
-        nc.vector.memset(placed[:].bitcast(I32), 0)
+        key_scales = pool.tile([P, H], U8, name="key_scales", align_bytes=64)
+        nc.vector.memset(d_bytes[:].bitcast(I32), 0)
+        nc.vector.memset(x_bytes[:].bitcast(I32), 0)
+        nc.vector.memset(key_scales[:].bitcast(I32), 0)
         ds = [pool.tile([P, 2 * S], F32, name=f"ds{u}") for u in range(TILES)]
         for u in range(TILES):
             nc.vector.memset(ds[u][:, S:], 0.0)
@@ -49,18 +51,13 @@ def tile_picked_kmixirelay_none_p_kernel(
         x_tab = pool.tile([P, T], I32, name="x_tab", align_bytes=64)
         gain = pool.tile([P, PACK], F32, name="gain")
 
-        def load_scale_rows(table, scales):
-            rows = scales[0].bitcast(I32)
-            nc.sync.dma_start(table[:].bitcast(I32), rows.unsqueeze(1).to_broadcast([16, 8, rows.shape[1]]))
-
         nc.sync.dma_start(k1_t[:], k1)
-        load_scale_rows(d_bytes, d_scales)
         nc.sync.dma_start(offs_t[:], offs)
         nc.sync.dma_start(two_t[:], two)
-        load_scale_rows(x_bytes, x_scales)
+        nc.sync.dma_start(d_bytes[0:P:8, :].bitcast(I32), d_scales[0].bitcast(I32))
         nc.sync.dma_start(d_tab[:], d_words[0].rearrange("p n t -> p (n t)").bitcast(I32))
-        nc.sync.dma_start(n1_t[:], n1)
-        nc.sync.dma_start(n2_t[:], n2)
+        for q in range(4):
+            nc.sync.dma_start(x_bytes[32 * q : 32 * q + 4, :].bitcast(I32), x_scales[0, 4 * q : 4 * q + 4].bitcast(I32))
         nc.sync.dma_start(x_tab[:], x_words[0].rearrange("p n t -> p (n t)").bitcast(I32))
         nc.gpsimd.dma_start(gain[:], gn.rearrange("(p t) o -> p (t o)", t=PACK))
 
@@ -73,8 +70,8 @@ def tile_picked_kmixirelay_none_p_kernel(
 
         load_w(0, 0)
 
-        picked = pool.tile([P, H + 2 * S], U8, name="picked", align_bytes=64)
-        dealt = pool.tile([P, H + 2 * S], U8, name="dealt", align_bytes=64)
+        picked = pool.tile([P, H], U8, name="picked", align_bytes=64)
+        dealt = pool.tile([P, H], U8, name="dealt", align_bytes=64)
 
         def gather_keys(table, gathered, target, run):
             for b in range(2):
@@ -87,32 +84,32 @@ def tile_picked_kmixirelay_none_p_kernel(
                     gathered[:, b * H // 2 : (b + 1) * H // 2].rearrange("p (c i t) -> p c t i", t=PACK, i=run),
                 )
 
-        gather_keys(d_bytes[:], picked[:, 0:H], dealt[:, 0:H], 16)
-        nc.vector.tensor_copy(picked[:, H : H + S], x_bytes[:].indirect(offs_t[:]))
-        nc.vector.tensor_copy(picked[:, H + S :], x_bytes[:].indirect(two_t[:]))
-        nc.vector.tensor_copy(dealt[:, H:].bitcast(I32), picked[:, H:].bitcast(I32))
+        gather_keys(d_bytes[:], picked[:], dealt[:], 16)
         for a in range(PACK):
-            queue = nc.sync if a % 2 == 0 else nc.scalar
-            queue.dma_start(placed[a:P:32, :].bitcast(I32), dealt[8 * a : P : 32, :].bitcast(I32))
-
+            nc.sync.dma_start(key_scales[a:P:32, :].bitcast(I32), dealt[8 * a : P : 32, :].bitcast(I32))
         load_w(0, 1)
-        for u in range(1, TILES):
+        load_w(1, 0)
+        nc.sync.dma_start(n1_t[:], n1)
+        load_w(1, 1)
+        nc.sync.dma_start(n2_t[:], n2)
+        for u in range(2, TILES):
             load_w(u, 0)
             load_w(u, 1)
 
         keys = pool.tile([P, H], U32, name="keys", align_bytes=64)
         key_words = pool.tile([P, H], U32, name="key_words", align_bytes=64)
         gather_keys(d_tab[:].bitcast(U32), keys[:], key_words[:], 4)
+        xo_scales = pool.tile([P, S], U8, name="xo_scales", align_bytes=64)
+        xt_scales = pool.tile([P, S], U8, name="xt_scales", align_bytes=64)
+        nc.vector.tensor_copy(xo_scales[:], x_bytes[:].indirect(offs_t[:]))
+        nc.vector.tensor_copy(xt_scales[:], x_bytes[:].indirect(two_t[:]))
         xo = pool.tile([P, S], U32, name="xo", align_bytes=64)
         xt = pool.tile([P, S], U32, name="xt", align_bytes=64)
         halves = [slice(0, HALF), slice(HALF, S)]
         cols16 = [slice(0, HALF // 16), slice(HALF // 16, S // 16)]
         nc.vector.tensor_copy(xo[:, halves[0]], x_tab[:].bitcast(U32).indirect(offs_t[:, cols16[0]]))
-        key_scales = placed[:, 0:H]
         nc.vector.tensor_copy(xo[:, halves[1]], x_tab[:].bitcast(U32).indirect(offs_t[:, cols16[1]]))
         nc.vector.tensor_copy(xt[:], x_tab[:].bitcast(U32).indirect(two_t[:]))
-        xo_scales = placed[:, H : H + S]
-        xt_scales = placed[:, H + S :]
 
         s_banks = [psum.tile([P, PACK, HALF], F32, name=f"s{b}") for b in range(2)]
         for b in range(2):
@@ -130,25 +127,26 @@ def tile_picked_kmixirelay_none_p_kernel(
         w_bf = {}
         z_bf = {}
 
-        def staged(width, name, slot):
-            return pool.tile([P, width], BF16, name=name, tag=f"staged{slot}", align_bytes=64)
+        def staged(u):
+            w_bf[u] = pool.tile([P, 2 * P * PACK], BF16, name=f"w_bf{u}", tag=f"w_bf{min(u, 1)}", align_bytes=64)
 
         w_q = [pool.tile([P, 2 * P], U32, name=f"w_q{u}", tag=f"w_q{u}", align_bytes=64) for u in range(TILES)]
         w_s = [pool.tile([P, 2 * P], U8, name=f"w_s{u}", align_bytes=64) for u in range(TILES)]
 
         def cast(copy, u, i):
             copy(
-                w_bf[u, i].rearrange("p (c n j) -> p c j n", j=PACK, n=4),
+                w_bf[u][:, i * P * PACK : (i + 1) * P * PACK].rearrange("p (c n j) -> p c j n", j=PACK, n=4),
                 raw[u, i].rearrange("p j (c n) -> p c j n", n=4),
             )
 
-        def quantise_w(u, lo, hi, source):
-            nc.vector.quantize_mx(w_q[u][:, lo * P : hi * P].bitcast(FP8X4), w_s[u][:, lo * P : hi * P], source)
+        def quantise_w(u):
+            nc.vector.quantize_mx(w_q[u][:].bitcast(FP8X4), w_s[u][:], w_bf[u][:])
 
         z_q = pool.tile([P, S], U32, name="z_q", align_bytes=64)
         z_s = pool.tile([P, S], U8, name="z_s", align_bytes=64)
 
         def make_z(b):
+            z_bf[b] = pool.tile([P, HALF * PACK], BF16, name=f"z_bf{b}", align_bytes=64)[:]
             nc.vector.scalar_tensor_tensor(
                 z_bf[b].rearrange("p (n t) -> p n t", t=PACK),
                 s_banks[b][:].rearrange("p t n -> p n t"),
@@ -185,61 +183,55 @@ def tile_picked_kmixirelay_none_p_kernel(
                 stop=True,
             )
 
-        h = [pool.tile([P, S], F32, name=f"h{u}") for u in range(TILES)]
+        h = {u: pool.tile([P, S], F32, name=f"h{u}") for u in range(1, TILES)}
         fetched = {}
 
-        def fetch(u, tag):
+        def fetch(u, tag, pieces):
             fetched[u] = pool.tile([P, S], F32, name=f"fetched{u}", tag=tag)
-            nc.scalar.activation(fetched[u][:], ds[u][:].indirect(n2_t[:]), COPY)
+            for cols, entries in pieces:
+                nc.scalar.activation(fetched[u][:, cols], ds[u][:].indirect(n2_t[:, entries]), COPY)
 
-        def finish(u):
-            nc.vector.tensor_tensor(res[:, u * S : (u + 1) * S], h[u][:], fetched[u][:], MAX)
-            nc.sync.dma_start(out[u * P : (u + 1) * P, :], res[:, u * S : (u + 1) * S])
+        def finish(u, pieces):
+            for cols, entries in pieces:
+                nc.vector.tensor_tensor(res[:, u, cols], h[u][:, cols], fetched[u][:, cols], MAX)
+                nc.sync.dma_start(out[u * P : (u + 1) * P, cols], res[:, u, cols])
 
-        width = P * PACK
-        both = staged(2 * width, "w_bf0", 0)
-        w_bf[0, 0], w_bf[0, 1] = both[:, :width], both[:, width:]
-        z_bf[0] = staged(width, "z_bf0", 1)[:]
-        cast(nc.scalar.copy, 0, 0)
-        cast(nc.scalar.copy, 0, 1)
+        whole = [(slice(0, S), slice(0, S // 16))]
+        split = list(zip(halves, cols16))
+
+        for u in range(2):
+            staged(u)
+            cast(nc.scalar.copy, u, 0)
+            cast(nc.scalar.copy, u, 1)
+        h[0] = pool.tile([P, S], F32, name="h0", tag="raw11")
         make_z(0)
-        quantise_w(0, 0, 1, w_bf[0, 0])
-        quantise_z(0)
-        quantise_w(0, 1, 2, w_bf[0, 1])
-        first = [psum.tile([P, HALF], F32, name=f"first{b}") for b in range(2)]
-        product(first[0][:], 0, halves[0])
-        nc.scalar.copy(h[0][:, halves[0]], first[0][:])
-        nc.scalar.activation(ds[0][:].indirect(n1_t[:, cols16[0]]), h[0][:, halves[0]], COPY)
-        w_bf[1, 0] = staged(width, "w_bf10", 1)[:]
-        cast(nc.scalar.copy, 1, 0)
-        both = staged(2 * width, "z_bf1_w_bf11", 0)
-        z_bf[1], w_bf[1, 1] = both[:, :width], both[:, width:]
         make_z(1)
-        cast(nc.vector.tensor_copy, 1, 1)
+        quantise_z(0)
+        quantise_w(0)
         quantise_z(1)
-        product(first[1][:], 0, halves[1])
-        quantise_w(1, 0, 1, w_bf[1, 0])
-        quantise_w(1, 1, 2, w_bf[1, 1])
-        nc.vector.tensor_copy(h[0][:, halves[1]], first[1][:])
-        nc.scalar.activation(ds[0][:].indirect(n1_t[:, cols16[1]]), h[0][:, halves[1]], COPY)
+        quantise_w(1)
+        first = [psum.tile([P, HALF], F32, name=f"first{b}") for b in range(2)]
+        for b, copy in enumerate((nc.scalar.copy, nc.vector.tensor_copy)):
+            product(first[b][:], 0, halves[b])
+            copy(h[0][:, halves[b]], first[b][:])
+            nc.scalar.activation(ds[0][:].indirect(n1_t[:, cols16[b]]), h[0][:, halves[b]], COPY)
         for u in range(1, TILES):
             acc = psum.tile([P, S], F32, name=f"acc{u}")
             product(acc[:], u, slice(0, S))
             if u + 1 < TILES:
-                both = staged(2 * width, f"w_bf{u + 1}", 0)
-                w_bf[u + 1, 0], w_bf[u + 1, 1] = both[:, :width], both[:, width:]
+                staged(u + 1)
                 cast(nc.vector.tensor_copy, u + 1, 0)
             nc.vector.tensor_copy(h[u][:], acc[:])
             if u + 1 < TILES:
                 cast(nc.vector.tensor_copy, u + 1, 1)
-                quantise_w(u + 1, 0, 2, both[:])
+                quantise_w(u + 1)
             nc.scalar.activation(ds[u][:].indirect(n1_t[:]), h[u][:], COPY)
             if u + 1 < TILES:
-                fetch(u - 1, f"raw{u + 1}1")
-        res = pool.tile([P, TILES * S], F32, name="res", tag=f"w_q{TILES - 1}", align_bytes=64)
-        finish(0)
-        fetch(2, "raw21")
-        finish(1)
-        fetch(3, "raw31")
-        finish(2)
-        finish(3)
+                fetch(u - 1, f"raw{u + 1}1", whole)
+        res = pool.tile([P, TILES, S], F32, name="res", tag=f"w_q{TILES - 1}", align_bytes=64)
+        finish(0, whole)
+        fetch(2, "raw21", whole)
+        finish(1, whole)
+        fetch(3, "raw31", split)
+        finish(2, whole)
+        finish(3, split)

@@ -68,8 +68,6 @@ def tile_picked_kmixirelay_none_p_kernel(
             w = (w2, w1)[i]
             nc.sync.dma_start(raw[u, i], w[:, u * P : (u + 1) * P].rearrange("(p j) n -> p j n", j=PACK))
 
-        load_w(0, 0)
-
         picked = pool.tile([P, H], U8, name="picked", align_bytes=64)
         dealt = pool.tile([P, H], U8, name="dealt", align_bytes=64)
 
@@ -87,10 +85,11 @@ def tile_picked_kmixirelay_none_p_kernel(
         gather_keys(d_bytes[:], picked[:], dealt[:], 16)
         for a in range(PACK):
             nc.sync.dma_start(key_scales[a:P:32, :].bitcast(I32), dealt[8 * a : P : 32, :].bitcast(I32))
+        load_w(0, 0)
         load_w(0, 1)
         load_w(1, 0)
-        nc.sync.dma_start(n1_t[:], n1)
         load_w(1, 1)
+        nc.sync.dma_start(n1_t[:], n1)
         nc.sync.dma_start(n2_t[:], n2)
         for u in range(2, TILES):
             load_w(u, 0)
@@ -146,7 +145,7 @@ def tile_picked_kmixirelay_none_p_kernel(
         z_s = pool.tile([P, S], U8, name="z_s", align_bytes=64)
 
         def make_z(b):
-            z_bf[b] = pool.tile([P, HALF * PACK], BF16, name=f"z_bf{b}", align_bytes=64)[:]
+            z_bf[b] = pool.tile([P, HALF * PACK], BF16, name=f"z_bf{b}", tag=("z_bf0", "w_bf0")[b], align_bytes=64)[:]
             nc.vector.scalar_tensor_tensor(
                 z_bf[b].rearrange("p (n t) -> p n t", t=PACK),
                 s_banks[b][:].rearrange("p t n -> p n t"),
@@ -205,9 +204,9 @@ def tile_picked_kmixirelay_none_p_kernel(
             cast(nc.scalar.copy, u, 1)
         h[0] = pool.tile([P, S], F32, name="h0", tag="raw11")
         make_z(0)
-        make_z(1)
-        quantise_z(0)
         quantise_w(0)
+        quantise_z(0)
+        make_z(1)
         quantise_z(1)
         quantise_w(1)
         first = [psum.tile([P, HALF], F32, name=f"first{b}") for b in range(2)]

@@ -68,6 +68,8 @@ def tile_picked_kmixirelay_none_p_kernel(
             w = (w2, w1)[i]
             nc.sync.dma_start(raw[u, i], w[:, u * P : (u + 1) * P].rearrange("(p j) n -> p j n", j=PACK))
 
+        load_w(0, 0)
+
         picked = pool.tile([P, H], U8, name="picked", align_bytes=64)
         dealt = pool.tile([P, H], U8, name="dealt", align_bytes=64)
 
@@ -85,11 +87,10 @@ def tile_picked_kmixirelay_none_p_kernel(
         gather_keys(d_bytes[:], picked[:], dealt[:], 16)
         for a in range(PACK):
             nc.sync.dma_start(key_scales[a:P:32, :].bitcast(I32), dealt[8 * a : P : 32, :].bitcast(I32))
-        load_w(0, 0)
         load_w(0, 1)
+        nc.sync.dma_start(n1_t[:], n1)
         load_w(1, 0)
         load_w(1, 1)
-        nc.sync.dma_start(n1_t[:], n1)
         nc.sync.dma_start(n2_t[:], n2)
         for u in range(2, TILES):
             load_w(u, 0)
@@ -126,26 +127,28 @@ def tile_picked_kmixirelay_none_p_kernel(
         w_bf = {}
         z_bf = {}
 
-        def staged(u):
-            w_bf[u] = pool.tile([P, 2 * P * PACK], BF16, name=f"w_bf{u}", tag=f"w_bf{min(u, 1)}", align_bytes=64)
+        def staged(u, tag):
+            both = pool.tile([P, 2, P * PACK], BF16, name=f"w_bf{u}", tag=tag, align_bytes=64)
+            w_bf[u, 0], w_bf[u, 1] = both[:, 0], both[:, 1]
+            return both[:].rearrange("p i c -> p (i c)")
 
         w_q = [pool.tile([P, 2 * P], U32, name=f"w_q{u}", tag=f"w_q{u}", align_bytes=64) for u in range(TILES)]
-        w_s = [pool.tile([P, 2 * P], U8, name=f"w_s{u}", align_bytes=64) for u in range(TILES)]
+        w_s = [pool.tile([P, 2 * P], U8, name=f"w_s{u}", tag=f"w_s{u}", align_bytes=64) for u in range(TILES)]
 
         def cast(copy, u, i):
             copy(
-                w_bf[u][:, i * P * PACK : (i + 1) * P * PACK].rearrange("p (c n j) -> p c j n", j=PACK, n=4),
+                w_bf[u, i].rearrange("p (c n j) -> p c j n", j=PACK, n=4),
                 raw[u, i].rearrange("p j (c n) -> p c j n", n=4),
             )
 
-        def quantise_w(u):
-            nc.vector.quantize_mx(w_q[u][:].bitcast(FP8X4), w_s[u][:], w_bf[u][:])
+        def quantise_w(u, source, cols):
+            nc.vector.quantize_mx(w_q[u][:, cols].bitcast(FP8X4), w_s[u][:, cols], source)
 
         z_q = pool.tile([P, S], U32, name="z_q", align_bytes=64)
         z_s = pool.tile([P, S], U8, name="z_s", align_bytes=64)
 
         def make_z(b):
-            z_bf[b] = pool.tile([P, HALF * PACK], BF16, name=f"z_bf{b}", tag=("z_bf0", "w_bf0")[b], align_bytes=64)[:]
+            z_bf[b] = pool.tile([P, HALF * PACK], BF16, name=f"z_bf{b}", tag=f"z_bf{b}", align_bytes=64)[:]
             nc.vector.scalar_tensor_tensor(
                 z_bf[b].rearrange("p (n t) -> p n t", t=PACK),
                 s_banks[b][:].rearrange("p t n -> p n t"),
@@ -185,8 +188,7 @@ def tile_picked_kmixirelay_none_p_kernel(
         h = {u: pool.tile([P, S], F32, name=f"h{u}") for u in range(1, TILES)}
         fetched = {}
 
-        def fetch(u, tag, pieces):
-            fetched[u] = pool.tile([P, S], F32, name=f"fetched{u}", tag=tag)
+        def fetch(u, pieces):
             for cols, entries in pieces:
                 nc.scalar.activation(fetched[u][:, cols], ds[u][:].indirect(n2_t[:, entries]), COPY)
 
@@ -198,39 +200,50 @@ def tile_picked_kmixirelay_none_p_kernel(
         whole = [(slice(0, S), slice(0, S // 16))]
         split = list(zip(halves, cols16))
 
-        for u in range(2):
-            staged(u)
-            cast(nc.scalar.copy, u, 0)
-            cast(nc.scalar.copy, u, 1)
-        h[0] = pool.tile([P, S], F32, name="h0", tag="raw11")
+        staged(0, "w_bf0")
+        cast(nc.scalar.copy, 0, 0)
+        cast(nc.scalar.copy, 0, 1)
+        w_bf[1, 0] = pool.tile([P, P * PACK], BF16, name="w_bf10", align_bytes=64)[:]
+        cast(nc.scalar.copy, 1, 0)
+        h[0] = pool.tile([P, S], F32, name="h0", tag="raw10")
         make_z(0)
-        quantise_w(0)
-        quantise_z(0)
         make_z(1)
+        quantise_z(0)
+        quantise_w(0, w_bf[0, 0], slice(0, P))
+        quantise_w(0, w_bf[0, 1], slice(P, 2 * P))
         quantise_z(1)
-        quantise_w(1)
+        quantise_w(1, w_bf[1, 0], slice(0, P))
+        w_bf[1, 1] = pool.tile([P, P * PACK], BF16, name="w_bf11", tag="z_bf1", align_bytes=64)[:]
+        cast(nc.vector.tensor_copy, 1, 1)
         first = [psum.tile([P, HALF], F32, name=f"first{b}") for b in range(2)]
         for b, copy in enumerate((nc.scalar.copy, nc.vector.tensor_copy)):
             product(first[b][:], 0, halves[b])
             copy(h[0][:, halves[b]], first[b][:])
             nc.scalar.activation(ds[0][:].indirect(n1_t[:, cols16[b]]), h[0][:, halves[b]], COPY)
+        quantise_w(1, w_bf[1, 1], slice(P, 2 * P))
         for u in range(1, TILES):
-            acc = psum.tile([P, S], F32, name=f"acc{u}")
+            acc = psum.tile([P, S], F32, name=f"acc{u}", tag=f"acc{min(u, 2)}")
             product(acc[:], u, slice(0, S))
             if u + 1 < TILES:
-                staged(u + 1)
+                both = staged(u + 1, "z_bf1")
                 cast(nc.vector.tensor_copy, u + 1, 0)
+            else:
+                fetched[1] = pool.tile([P, S], F32, name="fetched1", tag="w_q3", align_bytes=64)[:]
+                fetch(1, whole)
             nc.vector.tensor_copy(h[u][:], acc[:])
             if u + 1 < TILES:
                 cast(nc.vector.tensor_copy, u + 1, 1)
-                quantise_w(u + 1)
+                quantise_w(u + 1, both, slice(0, 2 * P))
             nc.scalar.activation(ds[u][:].indirect(n1_t[:]), h[u][:], COPY)
-            if u + 1 < TILES:
-                fetch(u - 1, f"raw{u + 1}1", whole)
-        res = pool.tile([P, TILES, S], F32, name="res", tag=f"w_q{TILES - 1}", align_bytes=64)
+            if u == 1:
+                fetched[0] = pool.tile([P, S], F32, name="fetched0", tag="raw21")[:]
+                fetch(0, whole)
+        res = pool.tile([P, TILES, S], F32, name="res", tag="w_s3", align_bytes=64)
         finish(0, whole)
-        fetch(2, "raw21", whole)
         finish(1, whole)
-        fetch(3, "raw31", split)
+        last = pool.tile([P, 2, S], F32, name="fetched23", tag="w_q3", align_bytes=64)
+        fetched[2], fetched[3] = last[:, 0], last[:, 1]
+        fetch(2, whole)
+        fetch(3, split)
         finish(2, whole)
         finish(3, split)

from contextlib import ExitStack

import concourse.mybir as mybir

K, T, S, N, G, H = 512, 2048, 256, 512, 2048, 512
FLOPS = 2 * K * H * S + 2 * H * N * S + 2 * K * N * S

F32 = mybir.dt.float32
BF16 = mybir.dt.bfloat16
I32 = mybir.dt.int32
U32 = mybir.dt.uint32
U16 = mybir.dt.uint16
U8 = mybir.dt.uint8
FP8X4 = mybir.dt.float8_e4m3fn_x4
MULT = mybir.AluOpType.mult
MAX = mybir.AluOpType.max
COPY = mybir.ActivationFunctionType.Copy

P = 128
PACK = 4
HALF = S // 2
TILES = N // P


def tile_picked_kmixirelay_none_p_kernel(
    tc, x_words, x_scales, d_words, d_scales, gn, w1, w2, offs, k1, two, n1, n2, out
):
    nc = tc.nc
    with ExitStack() as ctx:
        lists = ctx.enter_context(tc.tile_pool(name="lists", bufs=1))
        pool = ctx.enter_context(tc.tile_pool(name="pool", bufs=1))
        psum = ctx.enter_context(tc.psum_pool(name="psum", bufs=1))

        k1_t = lists.tile([P, H // 16], U16, name="k1_t")
        offs_t = lists.tile([P, S // 16], U16, name="offs_t")
        two_t = lists.tile([P, S // 16], U16, name="two_t")
        n1_t = lists.tile([P, S // 16], U16, name="n1_t")
        n2_t = lists.tile([P, S // 16], U16, name="n2_t")

        d_bytes = pool.tile([P, G], U8, name="d_bytes", align_bytes=64)
        x_bytes = pool.tile([P, T], U8, name="x_bytes", align_bytes=64)
        key_scales = pool.tile([P, H], U8, name="key_scales", align_bytes=64)
        nc.vector.memset(d_bytes[:].bitcast(I32), 0)
        nc.vector.memset(x_bytes[:].bitcast(I32), 0)
        nc.vector.memset(key_scales[:].bitcast(I32), 0)
        ds = [pool.tile([P, 2 * S], F32, name=f"ds{u}") for u in range(TILES)]
        for u in range(TILES):
            nc.vector.memset(ds[u][:, S:], 0.0)

        d_tab = pool.tile([P, G], I32, name="d_tab", align_bytes=64)
        x_tab = pool.tile([P, T], I32, name="x_tab", align_bytes=64)
        gain = pool.tile([P, PACK], F32, name="gain")

        nc.sync.dma_start(k1_t[:], k1)
        nc.sync.dma_start(offs_t[:], offs)
        nc.sync.dma_start(two_t[:], two)
        nc.sync.dma_start(d_bytes[0:P:8, :].bitcast(I32), d_scales[0].bitcast(I32))
        nc.sync.dma_start(d_tab[:], d_words[0].rearrange("p n t -> p (n t)").bitcast(I32))
        for q in range(4):
            nc.sync.dma_start(x_bytes[32 * q : 32 * q + 4, :].bitcast(I32), x_scales[0, 4 * q : 4 * q + 4].bitcast(I32))
        nc.sync.dma_start(x_tab[:], x_words[0].rearrange("p n t -> p (n t)").bitcast(I32))
        nc.gpsimd.dma_start(gain[:], gn.rearrange("(p t) o -> p (t o)", t=PACK))

        raw = {}

        def load_w(u, i):
            raw[u, i] = pool.tile([P, PACK, P], F32, name=f"raw{u}{i}", tag=f"raw{u}{i}")[:]
            w = (w2, w1)[i]
            nc.sync.dma_start(raw[u, i], w[:, u * P : (u + 1) * P].rearrange("(p j) n -> p j n", j=PACK))

        load_w(0, 0)

        picked = pool.tile([P, H], U8, name="picked", align_bytes=64)
        dealt = pool.tile([P, H], U8, name="dealt", align_bytes=64)

        def gather_keys(table, gathered, target, run):
            for b in range(2):
                nc.vector.tensor_copy(
                    gathered[:, b * H // 2 : (b + 1) * H // 2], table.indirect(k1_t[:, b * H // 32 : (b + 1) * H // 32])
                )
            for b in range(2):
                nc.vector.tensor_copy(
                    target.rearrange("p (t b c i) -> p b c t i", t=PACK, b=2, i=run)[:, b],
                    gathered[:, b * H // 2 : (b + 1) * H // 2].rearrange("p (c i t) -> p c t i", t=PACK, i=run),
                )

        gather_keys(d_bytes[:], picked[:], dealt[:], 16)
        for a in range(PACK):
            nc.sync.dma_start(key_scales[a:P:32, :].bitcast(I32), dealt[8 * a : P : 32, :].bitcast(I32))
        load_w(0, 1)
        nc.sync.dma_start(n1_t[:], n1)
        load_w(1, 0)
        load_w(1, 1)
        nc.sync.dma_start(n2_t[:], n2)
        for u in range(2, TILES):
            load_w(u, 0)
            load_w(u, 1)

        keys = pool.tile([P, H], U32, name="keys", align_bytes=64)
        key_words = pool.tile([P, H], U32, name="key_words", align_bytes=64)
        gather_keys(d_tab[:].bitcast(U32), keys[:], key_words[:], 4)
        xo_scales = pool.tile([P, S], U8, name="xo_scales", align_bytes=64)
        xt_scales = pool.tile([P, S], U8, name="xt_scales", align_bytes=64)
        nc.vector.tensor_copy(xo_scales[:], x_bytes[:].indirect(offs_t[:]))
        nc.vector.tensor_copy(xt_scales[:], x_bytes[:].indirect(two_t[:]))
        xo = pool.tile([P, S], U32, name="xo", align_bytes=64)
        xt = pool.tile([P, S], U32, name="xt", align_bytes=64)
        halves = [slice(0, HALF), slice(HALF, S)]
        cols16 = [slice(0, HALF // 16), slice(HALF // 16, S // 16)]
        nc.vector.tensor_copy(xo[:, halves[0]], x_tab[:].bitcast(U32).indirect(offs_t[:, cols16[0]]))
        nc.vector.tensor_copy(xo[:, halves[1]], x_tab[:].bitcast(U32).indirect(offs_t[:, cols16[1]]))
        nc.vector.tensor_copy(xt[:], x_tab[:].bitcast(U32).indirect(two_t[:]))

        s_banks = [psum.tile([P, PACK, HALF], F32, name=f"s{b}") for b in range(2)]
        for b in range(2):
            for t in range(PACK):
                nc.tensor.matmul_mx(
                    s_banks[b][:, t, :],
                    lhsT=key_words[:, t * P : (t + 1) * P].bitcast(FP8X4),
                    lhsT_scale=key_scales[:, t * P : (t + 1) * P],
                    rhs=xo[:, halves[b]].bitcast(FP8X4),
                    rhs_scale=xo_scales[:, halves[b]],
                    start=True,
                    stop=True,
                )

        w_bf = {}
        z_bf = {}

        def staged(u, tag):
            both = pool.tile([P, 2, P * PACK], BF16, name=f"w_bf{u}", tag=tag, align_bytes=64)
            w_bf[u, 0], w_bf[u, 1] = both[:, 0], both[:, 1]
            return both[:].rearrange("p i c -> p (i c)")

        w_q = [pool.tile([P, 2 * P], U32, name=f"w_q{u}", tag=f"w_q{u}", align_bytes=64) for u in range(TILES)]
        w_s = [pool.tile([P, 2 * P], U8, name=f"w_s{u}", tag=f"w_s{u}", align_bytes=64) for u in range(TILES)]

        def cast(copy, u, i):
            copy(
                w_bf[u, i].rearrange("p (c n j) -> p c j n", j=PACK, n=4),
                raw[u, i].rearrange("p j (c n) -> p c j n", n=4),
            )

        def quantise_w(u, source, cols):
            nc.vector.quantize_mx(w_q[u][:, cols].bitcast(FP8X4), w_s[u][:, cols], source)

        z_q = pool.tile([P, S], U32, name="z_q", align_bytes=64)
        z_s = pool.tile([P, S], U8, name="z_s", align_bytes=64)

        def make_z(b):
            z_bf[b] = pool.tile([P, HALF * PACK], BF16, name=f"z_bf{b}", tag=f"z_bf{b}", align_bytes=64)[:]
            nc.vector.scalar_tensor_tensor(
                z_bf[b].rearrange("p (n t) -> p n t", t=PACK),
                s_banks[b][:].rearrange("p t n -> p n t"),
                0.0625,
                gain[:].unsqueeze(1).to_broadcast([P, HALF, PACK]),
                MULT,
                MULT,
            )

        def quantise_z(b):
            nc.vector.quantize_mx(
                z_q[:, halves[b]].bitcast(FP8X4),
                z_s[:, halves[b]],
                z_bf[b],
            )

        def product(acc, u, cols):
            nc.tensor.matmul_mx(
                acc,
                lhsT=w_q[u][:, 0:P].bitcast(FP8X4),
                lhsT_scale=w_s[u][:, 0:P],
                rhs=xt[:, cols].bitcast(FP8X4),
                rhs_scale=xt_scales[:, cols],
                start=True,
                stop=False,
            )
            nc.tensor.matmul_mx(
                acc,
                lhsT=w_q[u][:, P : 2 * P].bitcast(FP8X4),
                lhsT_scale=w_s[u][:, P : 2 * P],
                rhs=z_q[:, cols].bitcast(FP8X4),
                rhs_scale=z_s[:, cols],
                start=False,
                stop=True,
            )

        h = {u: pool.tile([P, S], F32, name=f"h{u}") for u in range(1, TILES)}
        fetched = {}

        def fetch(u, pieces):
            for cols, entries in pieces:
                nc.scalar.activation(fetched[u][:, cols], ds[u][:].indirect(n2_t[:, entries]), COPY)

        def finish(u, pieces):
            for cols, entries in pieces:
                nc.vector.tensor_tensor(res[:, u, cols], h[u][:, cols], fetched[u][:, cols], MAX)
                nc.sync.dma_start(out[u * P : (u + 1) * P, cols], res[:, u, cols])

        whole = [(slice(0, S), slice(0, S // 16))]
        split = list(zip(halves, cols16))

        staged(0, "w_bf0")
        cast(nc.scalar.copy, 0, 0)
        cast(nc.scalar.copy, 0, 1)
        w_bf[1, 0] = pool.tile([P, P * PACK], BF16, name="w_bf10", align_bytes=64)[:]
        cast(nc.scalar.copy, 1, 0)
        h[0] = pool.tile([P, S], F32, name="h0", tag="raw10")
        make_z(0)
        make_z(1)
        quantise_z(0)
        quantise_w(0, w_bf[0, 0], slice(0, P))
        quantise_w(0, w_bf[0, 1], slice(P, 2 * P))
        quantise_z(1)
        quantise_w(1, w_bf[1, 0], slice(0, P))
        w_bf[1, 1] = pool.tile([P, P * PACK], BF16, name="w_bf11", tag="z_bf1", align_bytes=64)[:]
        cast(nc.vector.tensor_copy, 1, 1)
        first = [psum.tile([P, HALF], F32, name=f"first{b}") for b in range(2)]
        for b, copy in enumerate((nc.scalar.copy, nc.vector.tensor_copy)):
            product(first[b][:], 0, halves[b])
            copy(h[0][:, halves[b]], first[b][:])
            nc.scalar.activation(ds[0][:].indirect(n1_t[:, cols16[b]]), h[0][:, halves[b]], COPY)
        quantise_w(1, w_bf[1, 1], slice(P, 2 * P))
        for u in range(1, TILES):
            acc = psum.tile([P, S], F32, name=f"acc{u}", tag=f"acc{min(u, 2)}")
            product(acc[:], u, slice(0, S))
            if u + 1 < TILES:
                both = staged(u + 1, "z_bf1")
                cast(nc.vector.tensor_copy, u + 1, 0)
            else:
                fetched[1] = pool.tile([P, S], F32, name="fetched1", tag="w_q3", align_bytes=64)[:]
                fetch(1, whole)
            nc.vector.tensor_copy(h[u][:], acc[:])
            if u + 1 < TILES:
                cast(nc.vector.tensor_copy, u + 1, 1)
                quantise_w(u + 1, both, slice(0, 2 * P))
            nc.scalar.activation(ds[u][:].indirect(n1_t[:]), h[u][:], COPY)
            if u == 1:
                fetched[0] = pool.tile([P, S], F32, name="fetched0", tag="raw21")[:]
                fetch(0, whole)
        res = pool.tile([P, TILES, S], F32, name="res", tag="w_s3", align_bytes=64)
        finish(0, whole)
        finish(1, whole)
        last = pool.tile([P, 2, S], F32, name="fetched23", tag="w_q3", align_bytes=64)
        fetched[2], fetched[3] = last[:, 0], last[:, 1]
        fetch(2, whole)
        fetch(3, split)
        finish(2, whole)
        finish(3, split)
